import numpy as np
import ml_dtypes


def mxq(x, axis, fmt="e4m3"):
    dtype, down = {"e4m3": (ml_dtypes.float8_e4m3fn, 7), "e5m2": (ml_dtypes.float8_e5m2, 14)}[fmt]
    v = np.moveaxis(np.asarray(x, np.float32).astype(ml_dtypes.bfloat16).astype(np.float64), axis, -1)
    blocks = v.reshape(v.shape[:-1] + (-1, 32))
    amax = np.abs(blocks).max(-1, keepdims=True)
    byte = np.maximum(np.where(amax > 0, np.frexp(amax)[1] - 1 + 127, 0) - down, 1)
    scale = np.exp2(byte - 127.0)
    codes = (blocks / scale).astype(np.float32).astype(dtype).astype(np.float64)
    return np.moveaxis((codes * scale).reshape(v.shape), -1, axis)


WIDE = False


def mx_kscale(k):
    if not WIDE:
        return np.ones(k)
    levels = np.array([30, -30])
    if k % 512:
        return np.exp2(np.random.permutation(np.resize(levels, k // 32))).repeat(32)
    a = np.empty((k // 512, 16))
    for p in range(k // 512):
        a[p, :8] = np.random.permutation(np.resize(levels, 8))
        for g in range(8):
            far = levels[np.abs(levels - a[p, g]) >= 10]
            a[p, g + 8] = far[np.random.randint(len(far))]
    return np.exp2(a.ravel()).repeat(32)


def f64(x):
    return np.asarray(x).astype(np.float64)


def striped(idx):
    return np.tile(np.asarray(idx).reshape(-1, 16).T, (8, 1)).astype(np.uint16)


def unstriped(offs):
    return offs[:16].T.reshape(-1).astype(np.int64)


E2M1 = np.array([0.0, 0.5, 1.0, 1.5, 2.0, 3.0, 4.0, 6.0, -0.0, -0.5, -1.0, -1.5, -2.0, -3.0, -4.0, -6.0])


def pack_weight(w, fmt):
    k, n = w.shape
    w = f64(np.asarray(w, np.float32).astype(ml_dtypes.bfloat16)).reshape(k // 32, 32, n)
    amax = np.abs(w).max(1)
    if fmt in ("e4m3", "e5m2"):
        byte = np.frexp(amax)[1] - 1 + 127 - (7 if fmt == "e4m3" else 14)
    else:
        mant, ex = np.frexp(amax / 6.0)
        byte = np.where(mant > 0.5, ex, ex - 1) + 127
    byte = np.clip(np.where(amax > 0, byte, 1), 1, 254)
    scaled = (w * np.exp2(127.0 - byte)[:, None, :]).reshape(k, n).astype(np.float32)
    by_word = np.ascontiguousarray(scaled.reshape(k // 512, 128, 4, n).transpose(0, 1, 3, 2))
    if fmt in ("e4m3", "e5m2"):
        words = by_word.astype(ml_dtypes.float8_e4m3fn if fmt == "e4m3" else ml_dtypes.float8_e5m2).view(np.uint8)
    else:
        c = by_word.astype(ml_dtypes.float4_e2m1fn).view(np.uint8) & 0xF
        words = (c[..., 0::2] | (c[..., 1::2] << 4)).reshape(k // 512, 128, 2 * n)
    return np.ascontiguousarray(words), np.ascontiguousarray(byte.astype(np.uint8).reshape(k // 512, 16, n))


def unpack_weight(words, scales, fmt):
    g, _, n = scales.shape
    words = np.ascontiguousarray(words).reshape(g, 128, n, -1)
    if fmt in ("e4m3", "e5m2"):
        vals = words.view(ml_dtypes.float8_e4m3fn if fmt == "e4m3" else ml_dtypes.float8_e5m2).astype(np.float64)
    else:
        nib = np.empty((g, 128, n, 4), np.uint8)
        nib[..., 0::2] = words & 0xF
        nib[..., 1::2] = words >> 4
        vals = E2M1[nib]
    vals = vals * np.repeat(np.exp2(scales.astype(np.float64) - 127.0), 8, axis=1)[..., None]
    return vals.transpose(0, 1, 3, 2).reshape(g * 512, n)


K, T, J, R, C, O, N, E = 512, 2048, 256, 512, 512, 256, 256, 1024


def setup_inputs():
    n = np.random.standard_normal
    idx = np.random.permutation(T)[:J]
    idx2 = np.random.permutation(T)[:J]
    idx3 = np.random.permutation(C)[:J]
    idx4 = np.random.permutation(C)[:J]
    idx5 = np.random.permutation(C)[:O]
    idx6 = np.random.permutation(C)[:O]
    idx7 = np.random.permutation(E)[:O]
    fk = mx_kscale(K)
    fr = mx_kscale(R)
    xtp = pack_weight(n((K, T)) / fk[:, None], "e4m3")
    wp = pack_weight(n((K, R)) * 1 / np.sqrt(K) * fk[:, None] * fr, "e2m1")
    wbp = pack_weight(n((R, N)) * 1 / np.sqrt(R) / fr[:, None], "e5m2")
    return {
        "xt_words": xtp[0],
        "xt_scales": xtp[1],
        "w_words": wp[0],
        "w_scales": wp[1],
        "sa": (np.random.uniform(0.5, 1.6, (R, 1))).astype(np.float32),
        "wb_words": wbp[0],
        "wb_scales": wbp[1],
        "tz": (np.random.randint(-9, 10, (N, E)).astype(np.float64)).astype(np.float32),
        "so": (np.random.uniform(0.1, 0.3, (N, 1))).astype(np.float32),
        "offs": striped(idx),
        "offs2": striped(idx2),
        "offs3": striped(idx3),
        "offs4": striped(idx4),
        "offs5": striped(idx5),
        "offs6": striped(idx6),
        "offs7": striped(idx7),
    }


def reference(xt_words, xt_scales, w_words, w_scales, sa, wb_words, wb_scales, tz, so, offs, offs2, offs3, offs4, offs5, offs6, offs7):
    idx = unstriped(offs)
    idx2 = unstriped(offs2)
    idx3 = unstriped(offs3)
    idx4 = unstriped(offs4)
    idx5 = unstriped(offs5)
    idx6 = unstriped(offs6)
    idx7 = unstriped(offs7)
    xtu = unpack_weight(xt_words, xt_scales, "e4m3")
    wu = unpack_weight(w_words, w_scales, "e2m1")
    wbu = unpack_weight(wb_words, wb_scales, "e5m2")
    xtidxg = xtu[:, idx]
    a = wu.T @ xtidxg
    xtidx2g = xtu[:, idx2]
    b = wu.T @ xtidx2g
    pw = np.zeros((R, C))
    pw[:, idx3] = a
    pv = np.zeros((R, C))
    pv[:, idx4] = b
    pg = pw + pv
    hid = np.maximum(pg[:, idx5] * f64(sa), pg[:, idx6])
    hidq = mxq(hid, 0, "e4m3")
    p = wbu.T @ hidq
    y = np.maximum(p, f64(tz)[:, idx7] * f64(so))
    return y

@@ -1,0 +1,199 @@
+from contextlib import ExitStack
+
+import concourse.mybir as mybir
+
+K, T, J, R, C, O, N, E = 512, 2048, 256, 512, 512, 256, 256, 1024
+FLOPS = 2 * K * R * J * 2 + 2 * R * N * O
+
+F32 = mybir.dt.float32
+BF16 = mybir.dt.bfloat16
+I32 = mybir.dt.int32
+U32 = mybir.dt.uint32
+U16 = mybir.dt.uint16
+U8 = mybir.dt.uint8
+E4M3 = mybir.dt.float8_e4m3fn_x4
+E5M2 = mybir.dt.float8_e5m2_x4
+E2M1 = mybir.dt.float4_e2m1fn_x4
+COPY = mybir.ActivationFunctionType.Copy
+ADD = mybir.AluOpType.add
+MAX = mybir.AluOpType.max
+
+P = 128
+PACK = 4
+QUADS = 4
+
+
+def tile_list_sumboardweighed_tied_one_stepfloor_kernel(
+    tc, xt_words, xt_scales, w_words, w_scales, sa, wb_words, wb_scales, tz, so,
+    offs, offs2, offs3, offs4, offs5, offs6, offs7, out,
+):
+    nc = tc.nc
+    with ExitStack() as ctx:
+        lists = ctx.enter_context(tc.tile_pool(name="lists", bufs=1))
+        keep = ctx.enter_context(tc.tile_pool(name="keep", bufs=1))
+        psum = ctx.enter_context(tc.psum_pool(name="psum", bufs=1))
+
+        def load_list(src, name):
+            tile = lists.tile([P, 16], U16, name=name)
+            nc.sync.dma_start(tile[:], src)
+            return tile
+
+        def load_scale_rows(plane, src):
+            for q in range(QUADS):
+                nc.sync.dma_start(
+                    plane[32 * q : 32 * q + 4, :].bitcast(I32), src[0, 4 * q : 4 * q + 4, :].bitcast(I32)
+                )
+
+        x_scales = keep.tile([P, T], U8, name="x_scales", tag="x_scales", align_bytes=64)
+        nc.vector.memset(x_scales[:].bitcast(I32), 0)
+
+        list_a = load_list(offs, "list_a")
+        w_raw = keep.tile([P, 2 * R], U8, name="w_raw", align_bytes=64)
+        nc.scalar.dma_start(w_raw[:].bitcast(I32), w_words[0].bitcast(I32))
+        w_scale_rows = keep.tile([4, QUADS, R], U8, name="w_scale_rows", align_bytes=64)
+        nc.sync.dma_start(
+            w_scale_rows[:].bitcast(I32), w_scales[0].rearrange("(q r) c -> r q c", q=QUADS).bitcast(I32)
+        )
+        x_words = keep.tile([P, T], U32, name="x_words", tag="x_words", align_bytes=64)
+        nc.scalar.dma_start(x_words[:].bitcast(I32), xt_words[0].rearrange("p n t -> p (n t)").bitcast(I32))
+        load_scale_rows(x_scales, xt_scales)
+        list_b = load_list(offs2, "list_b")
+        put_a = load_list(offs3, "put_a")
+        put_b = load_list(offs4, "put_b")
+        pick_scaled = load_list(offs5, "pick_scaled")
+        pick_plain = load_list(offs6, "pick_plain")
+        sa_cols = keep.tile([P, PACK], F32, name="sa_cols")
+        nc.sync.dma_start(sa_cols[:], sa.rearrange("(p t) one -> p (t one)", t=PACK))
+
+        w_scale_plane = keep.tile([P, R], U8, name="w_scale_plane", align_bytes=64)
+        nc.vector.memset(w_scale_plane[:].bitcast(I32), 0)
+        wb_plane = keep.tile([P, N], U8, name="wb_plane", align_bytes=64)
+        nc.vector.memset(wb_plane[:].bitcast(I32), 0)
+        boards_a = [keep.tile([P, C], F32, name="board_a%d" % i) for i in range(2)]
+        boards_b = [keep.tile([P, C], F32, name="board_b%d" % i) for i in range(2)]
+        for i in range(2):
+            nc.vector.memset(boards_a[i][:], 0.0)
+            nc.vector.memset(boards_b[i][:], 0.0)
+
+        wb_codes = keep.tile([P, N], U32, name="wb_codes", align_bytes=64)
+        nc.sync.dma_start(wb_codes[:].bitcast(I32), wb_words[0].rearrange("p n t -> p (n t)").bitcast(I32))
+        load_scale_rows(wb_plane, wb_scales)
+        pick_floor = load_list(offs7, "pick_floor")
+        so_cols = keep.tile([P, N // P], F32, name="so_cols")
+        with nc.allow_non_contiguous_dma(reason="one value a partition"):
+            nc.sync.dma_start(so_cols[:], so.rearrange("(h p) one -> p (h one)", p=P))
+
+        for q in range(QUADS):
+            nc.vector.tensor_copy(
+                w_scale_plane[32 * q : 32 * q + 4, :].bitcast(I32), w_scale_rows[:, q, :].bitcast(I32)
+            )
+        w_codes = keep.tile([P, 2 * R], U8, name="w_codes", align_bytes=64)
+        nc.vector.tensor_copy(
+            w_codes[:].bitcast(U16).rearrange("p (t m) -> p t m", t=PACK),
+            w_raw[:].bitcast(U16).rearrange("p (m t) -> p t m", t=PACK),
+        )
+        w_plane = keep.tile([P, R], U8, name="w_plane", align_bytes=64)
+        nc.vector.tensor_copy(
+            w_plane[:].rearrange("p (t m) -> p t m", t=PACK),
+            w_scale_plane[:].rearrange("p (m t) -> p t m", t=PACK),
+        )
+
+        picked_scales = []
+        for name, tokens in (("a", list_a), ("b", list_b)):
+            plane = keep.tile([P, J], U8, name="xs_" + name, align_bytes=64)
+            nc.vector.tensor_copy(plane[:], x_scales[:].indirect(tokens[:]))
+            picked_scales.append(plane)
+        sums = []
+        for side, (name, tokens) in enumerate((("a", list_a), ("b", list_b))):
+            codes = keep.tile([P, J], U32, name="xw_" + name, align_bytes=64)
+            nc.vector.tensor_copy(codes[:], x_words[:].indirect(tokens[:]))
+            banks = []
+            for t in range(PACK):
+                bank = psum.tile([P, J], F32, name="sum_%s%d" % (name, t), tag="bank%d" % (PACK * side + t))
+                nc.tensor.matmul_mx(
+                    out=bank[:],
+                    lhsT=w_codes[:, 2 * P * t : 2 * P * (t + 1)].bitcast(E2M1),
+                    lhsT_scale=w_plane[:, P * t : P * (t + 1)],
+                    rhs=codes[:].bitcast(E4M3),
+                    rhs_scale=picked_scales[side][:],
+                    start=True,
+                    stop=True,
+                )
+                banks.append(bank)
+            sums.append(banks)
+
+        floors = []
+        for h, tag in enumerate(("x_scales", "x_words")):
+            rows = keep.tile([P, E], F32, name="tz%d" % h, tag=tag, align_bytes=64)
+            nc.sync.dma_start(rows[:], tz[P * h : P * (h + 1), :])
+            floors.append(rows)
+
+        scaled = keep.tile([P, PACK, O], F32, name="scaled")
+        plain = keep.tile([P, PACK, O], F32, name="plain")
+        hid = keep.tile([P, O, PACK], BF16, name="hid", align_bytes=64)
+        totals = [None] * PACK
+
+        def put(t):
+            a_vals = keep.tile([P, J], F32, name="a_vals%d" % t)
+            nc.scalar.activation(a_vals[:], sums[0][t][:], COPY)
+            b_vals = keep.tile([P, J], F32, name="b_vals%d" % t)
+            if t == 0:
+                nc.vector.tensor_copy(b_vals[:], sums[1][t][:])
+            else:
+                nc.scalar.activation(b_vals[:], sums[1][t][:], COPY)
+            nc.scalar.activation(boards_a[t % 2][:].indirect(put_a[:]), a_vals[:], COPY)
+            nc.vector.tensor_copy(boards_b[t % 2][:].indirect(put_b[:]), b_vals[:])
+
+        def add(t):
+            totals[t] = keep.tile([P, C], F32, name="total%d" % t)
+            nc.vector.tensor_tensor(totals[t][:], boards_a[t % 2][:], boards_b[t % 2][:], ADD)
+
+        def pick(t):
+            nc.scalar.activation(
+                scaled[:, t, :], totals[t][:].indirect(pick_scaled[:]), COPY, scale=sa_cols[:, t : t + 1]
+            )
+            if t == 1:
+                nc.scalar.activation(plain[:, t, :], totals[t][:].indirect(pick_plain[:]), COPY)
+            else:
+                nc.vector.tensor_copy(plain[:, t, :], totals[t][:].indirect(pick_plain[:]))
+
+        def larger(t0):
+            nc.vector.tensor_tensor(
+                hid[:, :, t0 : t0 + 2],
+                scaled[:, t0 : t0 + 2, :].rearrange("p t o -> p o t"),
+                plain[:, t0 : t0 + 2, :].rearrange("p t o -> p o t"),
+                MAX,
+            )
+
+        put(0)
+        add(0)
+        for t in range(1, PACK):
+            put(t)
+            pick(t - 1)
+            if t == 2:
+                larger(0)
+            add(t)
+        pick(PACK - 1)
+        larger(2)
+
+        hid_codes = keep.tile([P, O], U32, name="hid_codes", align_bytes=64)
+        hid_plane = keep.tile([P, O], U8, name="hid_plane", align_bytes=64)
+        nc.vector.quantize_mx(
+            out=hid_codes[:].bitcast(E4M3), scales=hid_plane[:], in_=hid[:].rearrange("p o t -> p (o t)")
+        )
+        for h in range(N // P):
+            floor = keep.tile([P, O], F32, name="floor%d" % h)
+            nc.scalar.activation(floor[:], floors[h][:].indirect(pick_floor[:]), COPY, scale=so_cols[:, h : h + 1])
+            bank = psum.tile([P, O], F32, name="prod%d" % h, tag="bank%d" % h)
+            nc.tensor.matmul_mx(
+                out=bank[:],
+                lhsT=wb_codes[:, P * h : P * (h + 1)].bitcast(E5M2),
+                lhsT_scale=wb_plane[:, P * h : P * (h + 1)],
+                rhs=hid_codes[:].bitcast(E4M3),
+                rhs_scale=hid_plane[:],
+                start=True,
+                stop=True,
+            )
+            result = keep.tile([P, O], F32, name="result%d" % h)
+            nc.vector.tensor_tensor(result[:], bank[:], floor[:], MAX)
+            nc.sync.dma_start(out[P * h : P * (h + 1), :], result[:])

@@ -62,18 +62,19 @@ def tile_list_sumboardweighed_tied_one_stepfloor_kernel(
         put_b = load_list(offs4, "put_b")
         pick_scaled = load_list(offs5, "pick_scaled")
         pick_plain = load_list(offs6, "pick_plain")
-        sa_cols = keep.tile([P, PACK], F32, name="sa_cols")
+        sa_cols = keep.tile([P, PACK], F32, name="sa_cols", tag="sa_cols")
         nc.sync.dma_start(sa_cols[:], sa.rearrange("(p t) one -> p (t one)", t=PACK))
 
         w_scale_plane = keep.tile([P, R], U8, name="w_scale_plane", align_bytes=64)
         nc.vector.memset(w_scale_plane[:].bitcast(I32), 0)
         wb_plane = keep.tile([P, N], U8, name="wb_plane", align_bytes=64)
         nc.vector.memset(wb_plane[:].bitcast(I32), 0)
-        boards_a = [keep.tile([P, C], F32, name="board_a%d" % i) for i in range(2)]
-        boards_b = [keep.tile([P, C], F32, name="board_b%d" % i) for i in range(2)]
+        boards = [[None, None], [None, None]]
         for i in range(2):
-            nc.vector.memset(boards_a[i][:], 0.0)
-            nc.vector.memset(boards_b[i][:], 0.0)
+            for side in range(2):
+                name = "board%d%d" % (side, i)
+                boards[side][i] = keep.tile([P, C], F32, name=name, tag=name, align_bytes=64)
+                nc.vector.memset(boards[side][i][:], 0.0)
 
         wb_codes = keep.tile([P, N], U32, name="wb_codes", align_bytes=64)
         nc.sync.dma_start(wb_codes[:].bitcast(I32), wb_words[0].rearrange("p n t -> p (n t)").bitcast(I32))
@@ -88,7 +89,7 @@ def tile_list_sumboardweighed_tied_one_stepfloor_kernel(
                 w_scale_plane[32 * q : 32 * q + 4, :].bitcast(I32), w_scale_rows[:, q, :].bitcast(I32)
             )
         w_codes = keep.tile([P, 2 * R], U8, name="w_codes", align_bytes=64)
-        nc.vector.tensor_copy(
+        nc.scalar.copy(
             w_codes[:].bitcast(U16).rearrange("p (t m) -> p t m", t=PACK),
             w_raw[:].bitcast(U16).rearrange("p (m t) -> p t m", t=PACK),
         )
@@ -103,24 +104,25 @@ def tile_list_sumboardweighed_tied_one_stepfloor_kernel(
             plane = keep.tile([P, J], U8, name="xs_" + name, align_bytes=64)
             nc.vector.tensor_copy(plane[:], x_scales[:].indirect(tokens[:]))
             picked_scales.append(plane)
-        sums = []
+        picked_codes = []
         for side, (name, tokens) in enumerate((("a", list_a), ("b", list_b))):
-            codes = keep.tile([P, J], U32, name="xw_" + name, align_bytes=64)
+            codes = keep.tile([P, J], U32, name="xw_" + name, tag=("x_scales", "xw_b")[side], align_bytes=64)
             nc.vector.tensor_copy(codes[:], x_words[:].indirect(tokens[:]))
-            banks = []
-            for t in range(PACK):
-                bank = psum.tile([P, J], F32, name="sum_%s%d" % (name, t), tag="bank%d" % (PACK * side + t))
+            picked_codes.append(codes)
+        sums = [[None] * PACK, [None] * PACK]
+        for t in range(PACK):
+            for side in range(2):
+                bank = psum.tile([P, J], F32, name="sum%d%d" % (side, t), tag="bank%d" % (PACK * side + t))
                 nc.tensor.matmul_mx(
                     out=bank[:],
                     lhsT=w_codes[:, 2 * P * t : 2 * P * (t + 1)].bitcast(E2M1),
                     lhsT_scale=w_plane[:, P * t : P * (t + 1)],
-                    rhs=codes[:].bitcast(E4M3),
+                    rhs=picked_codes[side][:].bitcast(E4M3),
                     rhs_scale=picked_scales[side][:],
                     start=True,
                     stop=True,
                 )
-                banks.append(bank)
-            sums.append(banks)
+                sums[side][t] = bank
 
         floors = []
         for h, tag in enumerate(("x_scales", "x_words")):
@@ -128,72 +130,81 @@ def tile_list_sumboardweighed_tied_one_stepfloor_kernel(
             nc.sync.dma_start(rows[:], tz[P * h : P * (h + 1), :])
             floors.append(rows)
 
-        scaled = keep.tile([P, PACK, O], F32, name="scaled")
-        plain = keep.tile([P, PACK, O], F32, name="plain")
-        hid = keep.tile([P, O, PACK], BF16, name="hid", align_bytes=64)
         totals = [None] * PACK
 
-        def put(t):
-            a_vals = keep.tile([P, J], F32, name="a_vals%d" % t)
-            nc.scalar.activation(a_vals[:], sums[0][t][:], COPY)
-            b_vals = keep.tile([P, J], F32, name="b_vals%d" % t)
-            if t == 0:
-                nc.vector.tensor_copy(b_vals[:], sums[1][t][:])
+        def put(side, t):
+            board = boards[side][t % 2]
+            places = (put_a, put_b)[side]
+            vals = keep.tile([P, J], F32, name="vals%d%d" % (side, t), tag="vals%d%d" % (side, t))
+            if side == 0:
+                nc.scalar.activation(vals[:], sums[side][t][:], COPY)
+                nc.scalar.activation(board[:].indirect(places[:]), vals[:], COPY)
             else:
-                nc.scalar.activation(b_vals[:], sums[1][t][:], COPY)
-            nc.scalar.activation(boards_a[t % 2][:].indirect(put_a[:]), a_vals[:], COPY)
-            nc.vector.tensor_copy(boards_b[t % 2][:].indirect(put_b[:]), b_vals[:])
+                nc.vector.tensor_copy(vals[:], sums[side][t][:])
+                nc.vector.tensor_copy(board[:].indirect(places[:]), vals[:])
 
         def add(t):
-            totals[t] = keep.tile([P, C], F32, name="total%d" % t)
-            nc.vector.tensor_tensor(totals[t][:], boards_a[t % 2][:], boards_b[t % 2][:], ADD)
+            totals[t] = keep.tile([P, C], F32, name="total%d" % t, tag="total%d" % t)
+            nc.gpsimd.tensor_tensor(totals[t][:], boards[0][t % 2][:], boards[1][t % 2][:], ADD)
 
-        def pick(t):
+        def pick(t, lo, hi):
+            cols = slice(lo // 16, hi // 16)
             nc.scalar.activation(
-                scaled[:, t, :], totals[t][:].indirect(pick_scaled[:]), COPY, scale=sa_cols[:, t : t + 1]
+                scaled[:, t, lo:hi], totals[t][:].indirect(pick_scaled[:, cols]), COPY, scale=sa_cols[:, t : t + 1]
             )
-            if t == 1:
-                nc.scalar.activation(plain[:, t, :], totals[t][:].indirect(pick_plain[:]), COPY)
+            if t != 2:
+                nc.vector.tensor_copy(plain[:, t, lo:hi], totals[t][:].indirect(pick_plain[:, cols]))
             else:
-                nc.vector.tensor_copy(plain[:, t, :], totals[t][:].indirect(pick_plain[:]))
+                nc.scalar.activation(plain[:, t, lo:hi], totals[t][:].indirect(pick_plain[:, cols]), COPY)
 
-        def larger(t0):
+        def larger(t0, lo, hi):
             nc.vector.tensor_tensor(
-                hid[:, :, t0 : t0 + 2],
-                scaled[:, t0 : t0 + 2, :].rearrange("p t o -> p o t"),
-                plain[:, t0 : t0 + 2, :].rearrange("p t o -> p o t"),
+                hid[:, lo:hi, t0 : t0 + 2],
+                scaled[:, t0 : t0 + 2, lo:hi].rearrange("p t o -> p o t"),
+                plain[:, t0 : t0 + 2, lo:hi].rearrange("p t o -> p o t"),
                 MAX,
             )
 
-        put(0)
-        add(0)
-        for t in range(1, PACK):
-            put(t)
-            pick(t - 1)
-            if t == 2:
-                larger(0)
+        for t in range(PACK):
+            put(0, t)
+            put(1, t)
             add(t)
-        pick(PACK - 1)
-        larger(2)
+        scaled = keep.tile([P, PACK, O], F32, name="scaled", tag="vals03")
+        plain = keep.tile([P, PACK, O], F32, name="plain", tag="vals13")
+        hid = keep.tile([P, O, PACK], BF16, name="hid", align_bytes=64)
+        pick(0, 0, O)
+        pick(1, 0, O)
+        larger(0, 0, O)
 
         hid_codes = keep.tile([P, O], U32, name="hid_codes", align_bytes=64)
         hid_plane = keep.tile([P, O], U8, name="hid_plane", align_bytes=64)
-        nc.vector.quantize_mx(
-            out=hid_codes[:].bitcast(E4M3), scales=hid_plane[:], in_=hid[:].rearrange("p o t -> p (o t)")
-        )
+        halves = [(lo, lo + P) for lo in range(0, O, P)]
+        pick(2, 0, O)
+        for lo, hi in halves:
+            pick(3, lo, hi)
+            larger(2, lo, hi)
+        floor = keep.tile([P, N // P, O], F32, name="floor", tag="sa_cols")
         for h in range(N // P):
-            floor = keep.tile([P, O], F32, name="floor%d" % h)
-            nc.scalar.activation(floor[:], floors[h][:].indirect(pick_floor[:]), COPY, scale=so_cols[:, h : h + 1])
-            bank = psum.tile([P, O], F32, name="prod%d" % h, tag="bank%d" % h)
-            nc.tensor.matmul_mx(
-                out=bank[:],
-                lhsT=wb_codes[:, P * h : P * (h + 1)].bitcast(E5M2),
-                lhsT_scale=wb_plane[:, P * h : P * (h + 1)],
-                rhs=hid_codes[:].bitcast(E4M3),
-                rhs_scale=hid_plane[:],
-                start=True,
-                stop=True,
+            nc.scalar.activation(
+                floor[:, h, :], floors[h][:].indirect(pick_floor[:]), COPY, scale=so_cols[:, h : h + 1]
             )
-            result = keep.tile([P, O], F32, name="result%d" % h)
-            nc.vector.tensor_tensor(result[:], bank[:], floor[:], MAX)
-            nc.sync.dma_start(out[P * h : P * (h + 1), :], result[:])
+        for half, (lo, hi) in enumerate(halves):
+            nc.vector.quantize_mx(
+                out=hid_codes[:, lo:hi].bitcast(E4M3),
+                scales=hid_plane[:, lo:hi],
+                in_=hid[:, lo:hi, :].rearrange("p o t -> p (o t)"),
+            )
+            bank = psum.tile([P, N // P, P], F32, name="prod%d" % half, tag="bank%d" % half)
+            for h in range(N // P):
+                nc.tensor.matmul_mx(
+                    out=bank[:, h, :],
+                    lhsT=wb_codes[:, P * h : P * (h + 1)].bitcast(E5M2),
+                    lhsT_scale=wb_plane[:, P * h : P * (h + 1)],
+                    rhs=hid_codes[:, lo:hi].bitcast(E4M3),
+                    rhs_scale=hid_plane[:, lo:hi],
+                    start=True,
+                    stop=True,
+                )
+            result = keep.tile([P, N // P, P], F32, name="result%d" % half)
+            nc.vector.tensor_tensor(result[:], bank[:], floor[:, :, lo:hi], MAX)
+            nc.sync.dma_start(out[:, lo:hi].rearrange("(h p) o -> p h o", p=P), result[:])

@@ -38,33 +38,39 @@ def tile_list_sumboardweighed_tied_one_stepfloor_kernel(
             nc.sync.dma_start(tile[:], src)
             return tile
 
-        def load_scale_rows(plane, src):
-            for q in range(QUADS):
-                nc.sync.dma_start(
-                    plane[32 * q : 32 * q + 4, :].bitcast(I32), src[0, 4 * q : 4 * q + 4, :].bitcast(I32)
-                )
+        def load_scale_rows(queue, plane, src, q):
+            queue.dma_start(plane[32 * q : 32 * q + 4, :].bitcast(I32), src[0, 4 * q : 4 * q + 4, :].bitcast(I32))
 
-        x_scales = keep.tile([P, T], U8, name="x_scales", tag="x_scales", align_bytes=64)
-        nc.vector.memset(x_scales[:].bitcast(I32), 0)
-
+        x_scale_rows = keep.tile([P, 2, T], U8, name="x_scale_rows", align_bytes=64)
+        for half, queue in enumerate((nc.sync, nc.scalar)):
+            queue.dma_start(
+                x_scale_rows[64 * half : 64 * half + 4, :, :].bitcast(I32),
+                xt_scales[0, 8 * half : 8 * half + 8, :].rearrange("(q r) c -> r q c", q=2).bitcast(I32),
+            )
         list_a = load_list(offs, "list_a")
-        w_raw = keep.tile([P, 2 * R], U8, name="w_raw", align_bytes=64)
-        nc.scalar.dma_start(w_raw[:].bitcast(I32), w_words[0].bitcast(I32))
         w_scale_rows = keep.tile([4, QUADS, R], U8, name="w_scale_rows", align_bytes=64)
-        nc.sync.dma_start(
+        nc.scalar.dma_start(
             w_scale_rows[:].bitcast(I32), w_scales[0].rearrange("(q r) c -> r q c", q=QUADS).bitcast(I32)
         )
+        list_b = load_list(offs2, "list_b")
+        w_raw = keep.tile([P, 2 * R], U8, name="w_raw", align_bytes=64)
+        nc.scalar.dma_start(w_raw[:].bitcast(I32), w_words[0].bitcast(I32))
         x_words = keep.tile([P, T], U32, name="x_words", tag="x_words", align_bytes=64)
         nc.scalar.dma_start(x_words[:].bitcast(I32), xt_words[0].rearrange("p n t -> p (n t)").bitcast(I32))
-        load_scale_rows(x_scales, xt_scales)
-        list_b = load_list(offs2, "list_b")
         put_a = load_list(offs3, "put_a")
         put_b = load_list(offs4, "put_b")
         pick_scaled = load_list(offs5, "pick_scaled")
         pick_plain = load_list(offs6, "pick_plain")
+        pick_floor = load_list(offs7, "pick_floor")
         sa_cols = keep.tile([P, PACK], F32, name="sa_cols", tag="sa_cols")
         nc.sync.dma_start(sa_cols[:], sa.rearrange("(p t) one -> p (t one)", t=PACK))
 
+        so_cols = keep.tile([P, N // P], F32, name="so_cols")
+        with nc.allow_non_contiguous_dma(reason="one value a partition"):
+            nc.sync.dma_start(so_cols[:], so.rearrange("(h p) one -> p (h one)", p=P))
+
+        x_scales = keep.tile([P, T], U8, name="x_scales", tag="x_scales", align_bytes=64)
+        nc.vector.memset(x_scales[:].bitcast(I32), 0)
         w_scale_plane = keep.tile([P, R], U8, name="w_scale_plane", align_bytes=64)
         nc.vector.memset(w_scale_plane[:].bitcast(I32), 0)
         wb_plane = keep.tile([P, N], U8, name="wb_plane", align_bytes=64)
@@ -76,14 +82,16 @@ def tile_list_sumboardweighed_tied_one_stepfloor_kernel(
                 boards[side][i] = keep.tile([P, C], F32, name=name, tag=name, align_bytes=64)
                 nc.vector.memset(boards[side][i][:], 0.0)
 
+        for q in range(QUADS):
+            load_scale_rows(nc.sync, wb_plane, wb_scales, q)
         wb_codes = keep.tile([P, N], U32, name="wb_codes", align_bytes=64)
         nc.sync.dma_start(wb_codes[:].bitcast(I32), wb_words[0].rearrange("p n t -> p (n t)").bitcast(I32))
-        load_scale_rows(wb_plane, wb_scales)
-        pick_floor = load_list(offs7, "pick_floor")
-        so_cols = keep.tile([P, N // P], F32, name="so_cols")
-        with nc.allow_non_contiguous_dma(reason="one value a partition"):
-            nc.sync.dma_start(so_cols[:], so.rearrange("(h p) one -> p (h one)", p=P))
 
+        for q in range(QUADS):
+            first = 64 * (q // 2)
+            nc.vector.tensor_copy(
+                x_scales[32 * q : 32 * q + 4, :].bitcast(I32), x_scale_rows[first : first + 4, q % 2, :].bitcast(I32)
+            )
         for q in range(QUADS):
             nc.vector.tensor_copy(
                 w_scale_plane[32 * q : 32 * q + 4, :].bitcast(I32), w_scale_rows[:, q, :].bitcast(I32)
@@ -94,7 +102,7 @@ def tile_list_sumboardweighed_tied_one_stepfloor_kernel(
             w_raw[:].bitcast(U16).rearrange("p (m t) -> p t m", t=PACK),
         )
         w_plane = keep.tile([P, R], U8, name="w_plane", align_bytes=64)
-        nc.vector.tensor_copy(
+        nc.gpsimd.tensor_copy(
             w_plane[:].rearrange("p (t m) -> p t m", t=PACK),
             w_scale_plane[:].rearrange("p (m t) -> p t m", t=PACK),
         )
@@ -147,15 +155,20 @@ def tile_list_sumboardweighed_tied_one_stepfloor_kernel(
             totals[t] = keep.tile([P, C], F32, name="total%d" % t, tag="total%d" % t)
             nc.gpsimd.tensor_tensor(totals[t][:], boards[0][t % 2][:], boards[1][t % 2][:], ADD)
 
-        def pick(t, lo, hi):
-            cols = slice(lo // 16, hi // 16)
+        def pick_times_sa(t, lo, hi):
             nc.scalar.activation(
-                scaled[:, t, lo:hi], totals[t][:].indirect(pick_scaled[:, cols]), COPY, scale=sa_cols[:, t : t + 1]
+                scaled[:, t, lo:hi],
+                totals[t][:].indirect(pick_scaled[:, lo // 16 : hi // 16]),
+                COPY,
+                scale=sa_cols[:, t : t + 1],
             )
-            if t != 2:
-                nc.vector.tensor_copy(plain[:, t, lo:hi], totals[t][:].indirect(pick_plain[:, cols]))
+
+        def pick_as_is(t, lo, hi, on_vector):
+            window = totals[t][:].indirect(pick_plain[:, lo // 16 : hi // 16])
+            if on_vector:
+                nc.vector.tensor_copy(plain[:, t, lo:hi], window)
             else:
-                nc.scalar.activation(plain[:, t, lo:hi], totals[t][:].indirect(pick_plain[:, cols]), COPY)
+                nc.scalar.activation(plain[:, t, lo:hi], window, COPY)
 
         def larger(t0, lo, hi):
             nc.vector.tensor_tensor(
@@ -172,16 +185,19 @@ def tile_list_sumboardweighed_tied_one_stepfloor_kernel(
         scaled = keep.tile([P, PACK, O], F32, name="scaled", tag="vals03")
         plain = keep.tile([P, PACK, O], F32, name="plain", tag="vals13")
         hid = keep.tile([P, O, PACK], BF16, name="hid", align_bytes=64)
-        pick(0, 0, O)
-        pick(1, 0, O)
+        for t in range(2):
+            pick_times_sa(t, 0, O)
+            pick_as_is(t, 0, O, True)
         larger(0, 0, O)
 
         hid_codes = keep.tile([P, O], U32, name="hid_codes", align_bytes=64)
         hid_plane = keep.tile([P, O], U8, name="hid_plane", align_bytes=64)
         halves = [(lo, lo + P) for lo in range(0, O, P)]
-        pick(2, 0, O)
+        pick_times_sa(2, 0, O)
         for lo, hi in halves:
-            pick(3, lo, hi)
+            pick_times_sa(3, lo, hi)
+            pick_as_is(2, lo, hi, lo == 0)
+            pick_as_is(3, lo, hi, True)
             larger(2, lo, hi)
         floor = keep.tile([P, N // P, O], F32, name="floor", tag="sa_cols")
         for h in range(N // P):

@@ -80,7 +80,7 @@ def tile_list_sumboardweighed_tied_one_stepfloor_kernel(
             for side in range(2):
                 name = "board%d%d" % (side, i)
                 boards[side][i] = keep.tile([P, C], F32, name=name, tag=name, align_bytes=64)
-                nc.vector.memset(boards[side][i][:], 0.0)
+                (nc.vector, nc.gpsimd)[i].memset(boards[side][i][:], 0.0)
 
         for q in range(QUADS):
             load_scale_rows(nc.sync, wb_plane, wb_scales, q)
@@ -108,13 +108,12 @@ def tile_list_sumboardweighed_tied_one_stepfloor_kernel(
         )
 
         picked_scales = []
+        picked_codes = []
         for name, tokens in (("a", list_a), ("b", list_b)):
             plane = keep.tile([P, J], U8, name="xs_" + name, align_bytes=64)
             nc.vector.tensor_copy(plane[:], x_scales[:].indirect(tokens[:]))
             picked_scales.append(plane)
-        picked_codes = []
-        for side, (name, tokens) in enumerate((("a", list_a), ("b", list_b))):
-            codes = keep.tile([P, J], U32, name="xw_" + name, tag=("x_scales", "xw_b")[side], align_bytes=64)
+            codes = keep.tile([P, J], U32, name="xw_" + name, align_bytes=64)
             nc.vector.tensor_copy(codes[:], x_words[:].indirect(tokens[:]))
             picked_codes.append(codes)
         sums = [[None] * PACK, [None] * PACK]
@@ -194,9 +193,9 @@ def tile_list_sumboardweighed_tied_one_stepfloor_kernel(
         hid_plane = keep.tile([P, O], U8, name="hid_plane", align_bytes=64)
         halves = [(lo, lo + P) for lo in range(0, O, P)]
         pick_times_sa(2, 0, O)
+        pick_as_is(2, 0, O, False)
         for lo, hi in halves:
             pick_times_sa(3, lo, hi)
-            pick_as_is(2, lo, hi, lo == 0)
             pick_as_is(3, lo, hi, True)
             larger(2, lo, hi)
         floor = keep.tile([P, N // P, O], F32, name="floor", tag="sa_cols")

from contextlib import ExitStack

import concourse.mybir as mybir

K, T, J, R, C, O, N, E = 512, 2048, 256, 512, 512, 256, 256, 1024
FLOPS = 2 * K * R * J * 2 + 2 * R * N * O

F32 = mybir.dt.float32
BF16 = mybir.dt.bfloat16
I32 = mybir.dt.int32
U32 = mybir.dt.uint32
U16 = mybir.dt.uint16
U8 = mybir.dt.uint8
E4M3 = mybir.dt.float8_e4m3fn_x4
E5M2 = mybir.dt.float8_e5m2_x4
E2M1 = mybir.dt.float4_e2m1fn_x4
COPY = mybir.ActivationFunctionType.Copy
ADD = mybir.AluOpType.add
MAX = mybir.AluOpType.max

P = 128
PACK = 4
QUADS = 4


def tile_list_sumboardweighed_tied_one_stepfloor_kernel(
    tc, xt_words, xt_scales, w_words, w_scales, sa, wb_words, wb_scales, tz, so,
    offs, offs2, offs3, offs4, offs5, offs6, offs7, out,
):
    nc = tc.nc
    with ExitStack() as ctx:
        lists = ctx.enter_context(tc.tile_pool(name="lists", bufs=1))
        keep = ctx.enter_context(tc.tile_pool(name="keep", bufs=1))
        psum = ctx.enter_context(tc.psum_pool(name="psum", bufs=1))

        def load_list(src, name):
            tile = lists.tile([P, 16], U16, name=name)
            nc.sync.dma_start(tile[:], src)
            return tile

        def load_scale_rows(queue, plane, src, q):
            queue.dma_start(plane[32 * q : 32 * q + 4, :].bitcast(I32), src[0, 4 * q : 4 * q + 4, :].bitcast(I32))

        x_scale_rows = keep.tile([P, 2, T], U8, name="x_scale_rows", align_bytes=64)
        for half, queue in enumerate((nc.sync, nc.scalar)):
            queue.dma_start(
                x_scale_rows[64 * half : 64 * half + 4, :, :].bitcast(I32),
                xt_scales[0, 8 * half : 8 * half + 8, :].rearrange("(q r) c -> r q c", q=2).bitcast(I32),
            )
        list_a = load_list(offs, "list_a")
        w_scale_rows = keep.tile([4, QUADS, R], U8, name="w_scale_rows", align_bytes=64)
        nc.scalar.dma_start(
            w_scale_rows[:].bitcast(I32), w_scales[0].rearrange("(q r) c -> r q c", q=QUADS).bitcast(I32)
        )
        list_b = load_list(offs2, "list_b")
        w_raw = keep.tile([P, 2 * R], U8, name="w_raw", align_bytes=64)
        nc.scalar.dma_start(w_raw[:].bitcast(I32), w_words[0].bitcast(I32))
        x_words = keep.tile([P, T], U32, name="x_words", tag="x_words", align_bytes=64)
        nc.scalar.dma_start(x_words[:].bitcast(I32), xt_words[0].rearrange("p n t -> p (n t)").bitcast(I32))
        put_a = load_list(offs3, "put_a")
        put_b = load_list(offs4, "put_b")
        pick_scaled = load_list(offs5, "pick_scaled")
        pick_plain = load_list(offs6, "pick_plain")
        pick_floor = load_list(offs7, "pick_floor")
        sa_cols = keep.tile([P, PACK], F32, name="sa_cols", tag="sa_cols")
        nc.sync.dma_start(sa_cols[:], sa.rearrange("(p t) one -> p (t one)", t=PACK))

        so_cols = keep.tile([P, N // P], F32, name="so_cols")
        with nc.allow_non_contiguous_dma(reason="one value a partition"):
            nc.sync.dma_start(so_cols[:], so.rearrange("(h p) one -> p (h one)", p=P))

        x_scales = keep.tile([P, T], U8, name="x_scales", tag="x_scales", align_bytes=64)
        nc.vector.memset(x_scales[:].bitcast(I32), 0)
        w_scale_plane = keep.tile([P, R], U8, name="w_scale_plane", align_bytes=64)
        nc.vector.memset(w_scale_plane[:].bitcast(I32), 0)
        wb_plane = keep.tile([P, N], U8, name="wb_plane", align_bytes=64)
        nc.vector.memset(wb_plane[:].bitcast(I32), 0)
        boards = [[None, None], [None, None]]
        for i in range(2):
            for side in range(2):
                name = "board%d%d" % (side, i)
                boards[side][i] = keep.tile([P, C], F32, name=name, tag=name, align_bytes=64)
                (nc.vector, nc.gpsimd)[i].memset(boards[side][i][:], 0.0)

        for q in range(QUADS):
            load_scale_rows(nc.sync, wb_plane, wb_scales, q)
        wb_codes = keep.tile([P, N], U32, name="wb_codes", align_bytes=64)
        nc.sync.dma_start(wb_codes[:].bitcast(I32), wb_words[0].rearrange("p n t -> p (n t)").bitcast(I32))

        for q in range(QUADS):
            first = 64 * (q // 2)
            nc.vector.tensor_copy(
                x_scales[32 * q : 32 * q + 4, :].bitcast(I32), x_scale_rows[first : first + 4, q % 2, :].bitcast(I32)
            )
        for q in range(QUADS):
            nc.vector.tensor_copy(
                w_scale_plane[32 * q : 32 * q + 4, :].bitcast(I32), w_scale_rows[:, q, :].bitcast(I32)
            )
        w_codes = keep.tile([P, 2 * R], U8, name="w_codes", align_bytes=64)
        nc.scalar.copy(
            w_codes[:].bitcast(U16).rearrange("p (t m) -> p t m", t=PACK),
            w_raw[:].bitcast(U16).rearrange("p (m t) -> p t m", t=PACK),
        )
        w_plane = keep.tile([P, R], U8, name="w_plane", align_bytes=64)
        nc.gpsimd.tensor_copy(
            w_plane[:].rearrange("p (t m) -> p t m", t=PACK),
            w_scale_plane[:].rearrange("p (m t) -> p t m", t=PACK),
        )

        picked_scales = []
        picked_codes = []
        for name, tokens in (("a", list_a), ("b", list_b)):
            plane = keep.tile([P, J], U8, name="xs_" + name, align_bytes=64)
            nc.vector.tensor_copy(plane[:], x_scales[:].indirect(tokens[:]))
            picked_scales.append(plane)
            codes = keep.tile([P, J], U32, name="xw_" + name, align_bytes=64)
            nc.vector.tensor_copy(codes[:], x_words[:].indirect(tokens[:]))
            picked_codes.append(codes)
        sums = [[None] * PACK, [None] * PACK]
        for t in range(PACK):
            for side in range(2):
                bank = psum.tile([P, J], F32, name="sum%d%d" % (side, t), tag="bank%d" % (PACK * side + t))
                nc.tensor.matmul_mx(
                    out=bank[:],
                    lhsT=w_codes[:, 2 * P * t : 2 * P * (t + 1)].bitcast(E2M1),
                    lhsT_scale=w_plane[:, P * t : P * (t + 1)],
                    rhs=picked_codes[side][:].bitcast(E4M3),
                    rhs_scale=picked_scales[side][:],
                    start=True,
                    stop=True,
                )
                sums[side][t] = bank

        floors = []
        for h, tag in enumerate(("x_scales", "x_words")):
            rows = keep.tile([P, E], F32, name="tz%d" % h, tag=tag, align_bytes=64)
            nc.sync.dma_start(rows[:], tz[P * h : P * (h + 1), :])
            floors.append(rows)

        totals = [None] * PACK

        def put(side, t):
            board = boards[side][t % 2]
            places = (put_a, put_b)[side]
            vals = keep.tile([P, J], F32, name="vals%d%d" % (side, t), tag="vals%d%d" % (side, t))
            if side == 0:
                nc.scalar.activation(vals[:], sums[side][t][:], COPY)
                nc.scalar.activation(board[:].indirect(places[:]), vals[:], COPY)
            else:
                nc.vector.tensor_copy(vals[:], sums[side][t][:])
                nc.vector.tensor_copy(board[:].indirect(places[:]), vals[:])

        def add(t):
            totals[t] = keep.tile([P, C], F32, name="total%d" % t, tag="total%d" % t)
            nc.gpsimd.tensor_tensor(totals[t][:], boards[0][t % 2][:], boards[1][t % 2][:], ADD)

        def pick_times_sa(t, lo, hi):
            nc.scalar.activation(
                scaled[:, t, lo:hi],
                totals[t][:].indirect(pick_scaled[:, lo // 16 : hi // 16]),
                COPY,
                scale=sa_cols[:, t : t + 1],
            )

        def pick_as_is(t, lo, hi, on_vector):
            window = totals[t][:].indirect(pick_plain[:, lo // 16 : hi // 16])
            if on_vector:
                nc.vector.tensor_copy(plain[:, t, lo:hi], window)
            else:
                nc.scalar.activation(plain[:, t, lo:hi], window, COPY)

        def larger(t0, lo, hi):
            nc.vector.tensor_tensor(
                hid[:, lo:hi, t0 : t0 + 2],
                scaled[:, t0 : t0 + 2, lo:hi].rearrange("p t o -> p o t"),
                plain[:, t0 : t0 + 2, lo:hi].rearrange("p t o -> p o t"),
                MAX,
            )

        for t in range(PACK):
            put(0, t)
            put(1, t)
            add(t)
        scaled = keep.tile([P, PACK, O], F32, name="scaled", tag="vals03")
        plain = keep.tile([P, PACK, O], F32, name="plain", tag="vals13")
        hid = keep.tile([P, O, PACK], BF16, name="hid", align_bytes=64)
        for t in range(2):
            pick_times_sa(t, 0, O)
            pick_as_is(t, 0, O, True)
        larger(0, 0, O)

        hid_codes = keep.tile([P, O], U32, name="hid_codes", align_bytes=64)
        hid_plane = keep.tile([P, O], U8, name="hid_plane", align_bytes=64)
        halves = [(lo, lo + P) for lo in range(0, O, P)]
        pick_times_sa(2, 0, O)
        pick_as_is(2, 0, O, False)
        for lo, hi in halves:
            pick_times_sa(3, lo, hi)
            pick_as_is(3, lo, hi, True)
            larger(2, lo, hi)
        floor = keep.tile([P, N // P, O], F32, name="floor", tag="sa_cols")
        for h in range(N // P):
            nc.scalar.activation(
                floor[:, h, :], floors[h][:].indirect(pick_floor[:]), COPY, scale=so_cols[:, h : h + 1]
            )
        for half, (lo, hi) in enumerate(halves):
            nc.vector.quantize_mx(
                out=hid_codes[:, lo:hi].bitcast(E4M3),
                scales=hid_plane[:, lo:hi],
                in_=hid[:, lo:hi, :].rearrange("p o t -> p (o t)"),
            )
            bank = psum.tile([P, N // P, P], F32, name="prod%d" % half, tag="bank%d" % half)
            for h in range(N // P):
                nc.tensor.matmul_mx(
                    out=bank[:, h, :],
                    lhsT=wb_codes[:, P * h : P * (h + 1)].bitcast(E5M2),
                    lhsT_scale=wb_plane[:, P * h : P * (h + 1)],
                    rhs=hid_codes[:, lo:hi].bitcast(E4M3),
                    rhs_scale=hid_plane[:, lo:hi],
                    start=True,
                    stop=True,
                )
            result = keep.tile([P, N // P, P], F32, name="result%d" % half)
            nc.vector.tensor_tensor(result[:], bank[:], floor[:, :, lo:hi], MAX)
            nc.sync.dma_start(out[:, lo:hi].rearrange("(h p) o -> p h o", p=P), result[:])
